import numpy as np
import ml_dtypes


def mxq(x, axis, fmt="e4m3"):
    dtype, down = {"e4m3": (ml_dtypes.float8_e4m3fn, 7), "e5m2": (ml_dtypes.float8_e5m2, 14)}[fmt]
    v = np.moveaxis(np.asarray(x, np.float32).astype(ml_dtypes.bfloat16).astype(np.float64), axis, -1)
    blocks = v.reshape(v.shape[:-1] + (-1, 32))
    amax = np.abs(blocks).max(-1, keepdims=True)
    byte = np.maximum(np.where(amax > 0, np.frexp(amax)[1] - 1 + 127, 0) - down, 1)
    scale = np.exp2(byte - 127.0)
    codes = (blocks / scale).astype(np.float32).astype(dtype).astype(np.float64)
    return np.moveaxis((codes * scale).reshape(v.shape), -1, axis)


WIDE = False


def mx_kscale(k):
    if not WIDE:
        return np.ones(k)
    levels = np.array([10, -10, 5, -5, 0])
    if k % 512:
        return np.exp2(np.random.permutation(np.resize(levels, k // 32))).repeat(32)
    a = np.empty((k // 512, 16))
    for p in range(k // 512):
        a[p, :8] = np.random.permutation(np.resize(levels, 8))
        for g in range(8):
            far = levels[np.abs(levels - a[p, g]) >= 10]
            a[p, g + 8] = far[np.random.randint(len(far))]
    return np.exp2(a.ravel()).repeat(32)


def f64(x):
    return np.asarray(x).astype(np.float64)


def striped(idx):
    return np.tile(idx.reshape(-1, 16).T, (8, 1)).astype(np.uint16)


def unstriped(offs):
    return offs[:16].T.reshape(-1).astype(np.int64)


def gelu(v):
    return 0.5 * v * (1.0 + np.tanh(np.sqrt(2.0 / np.pi) * (v + 0.044715 * v**3)))


K, T, S, N = 512, 4096, 2048, 256


def setup_inputs():
    n = np.random.standard_normal
    s = mx_kscale(K)[:, None]
    return {
        "xT": (n((K, S)) * s).astype(np.float32),
        "w": (n((K, N)) / np.sqrt(K) / s).astype(np.float32),
        "b": (0.3 * n((N, 1))).astype(np.float32),
        "gate": np.tile(np.random.uniform(0.2, 1.0, S), (N, 1)).astype(np.float32),
        "offs": striped(np.sort(np.random.permutation(T)[:S])),
    }


def reference(xT, w, b, gate, offs):
    idx = unstriped(offs)
    xq = mxq(f64(xT), 0, "e4m3")
    y = mxq(f64(w), 0, "e4m3").T @ xq
    y = gelu(y + f64(b))
    out = np.zeros((N, T))
    out[:, idx] = f64(gate) * y
    return out

@@ -1,0 +1,168 @@
+from contextlib import ExitStack
+
+import concourse.mybir as mybir
+
+K, T, S, N = 512, 4096, 2048, 256
+FLOPS = 2 * K * S * N
+BYTES = 4 * (K * S + K * N + N + S + N * T) + 2 * S
+
+F32 = mybir.dt.float32
+BF16 = mybir.dt.bfloat16
+U32 = mybir.dt.uint32
+U16 = mybir.dt.uint16
+U8 = mybir.dt.uint8
+FP8X4 = mybir.dt.float8_e4m3fn_x4
+GELU = mybir.ActivationFunctionType.Gelu_apprx_tanh
+MULT = mybir.AluOpType.mult
+
+P = 128
+PACK = 4
+CHUNK = 512
+CHUNKS = S // CHUNK
+BLOCKS = N // P
+
+
+def tile_picked_place_lin_gelu_srt_l_kernel(tc, xT, w, b, gate, offs, out):
+    nc = tc.nc
+    with ExitStack() as ctx:
+        lists = ctx.enter_context(tc.tile_pool(name="lists", bufs=1))
+        keep = ctx.enter_context(tc.tile_pool(name="keep", bufs=1))
+        psum = ctx.enter_context(tc.psum_pool(name="psum", bufs=1))
+
+        offsets = lists.tile([P, S // 16], U16, name="offsets")
+
+        x_hbm = xT.rearrange("(p t) s -> p t s", t=PACK)
+        w_hbm = w.rearrange("(p t) m -> p t m", t=PACK)
+
+        pieces = [(0, 256), (256, 256), (512, 512), (1024, 512), (1536, 256), (1792, 256)]
+        raw = {c0: keep.tile([P, PACK, n], F32, name="raw%d" % c0) for c0, n in pieces}
+        codes = [keep.tile([P, CHUNK], U32, name="codes%d" % c, align_bytes=64) for c in range(CHUNKS)]
+        scales = [keep.tile([P, CHUNK], U8, name="scales%d" % c, align_bytes=64) for c in range(CHUNKS)]
+        gates = [keep.tile([P, CHUNK], F32, name="gate%d" % c) for c in range(CHUNKS)]
+        w_raw = keep.tile([P, PACK, N], F32, name="w_raw")
+        w_grouped = keep.tile([P, N * PACK], BF16, name="w_grouped", align_bytes=64)
+        w_codes = keep.tile([P, N], U32, name="w_codes", align_bytes=64)
+        w_scales = keep.tile([P, N], U8, name="w_scales", align_bytes=64)
+        bias = [keep.tile([P, 1], F32, name="bias%d" % k) for k in range(BLOCKS)]
+        windows = [keep.tile([P, T], F32, name="window%d" % k) for k in range(BLOCKS)]
+        small = keep.tile([P, 2], F32, name="small")
+
+        def load_x(c0):
+            n = raw[c0].shape[2]
+            nc.sync.dma_start(raw[c0][:], x_hbm[:, :, c0 : c0 + n])
+
+        def load_gate(c):
+            nc.sync.dma_start(gates[c][:], gate[0:P, c * CHUNK : (c + 1) * CHUNK])
+
+        load_x(0)
+        nc.sync.dma_start(w_raw[:], w_hbm)
+        load_x(256)
+        nc.sync.dma_start(offsets[:], offs)
+        load_gate(0)
+        load_x(512)
+        load_gate(1)
+        load_x(1024)
+        load_gate(2)
+        load_x(1536)
+        load_x(1792)
+        load_gate(3)
+        for k in range(BLOCKS):
+            nc.scalar.dma_start(bias[k][:], b[k * P : (k + 1) * P, :])
+
+        nc.gpsimd.memset(small[:, 0:1], 0.0)
+        nc.scalar.activation(out=small[:, 1:2], in_=small[:, 0:1], func=GELU)
+
+        def clear(k):
+            for q in range(4):
+                nc.vector.memset(windows[k][:, q * 1024 : (q + 1) * 1024], 0.0)
+
+        def interleave(copy, src, dst, a, e):
+            copy(
+                dst[:, PACK * a : PACK * e].rearrange("p (c i t) -> p c t i", i=4, t=PACK),
+                src[:, :, a:e].rearrange("p t (c i) -> p c t i", i=4),
+            )
+
+        def vec(dst, src):
+            nc.vector.tensor_copy(out=dst, in_=src)
+
+        def act(dst, src):
+            nc.scalar.copy(out=dst, in_=src)
+
+        def new_grouped(c0, tag):
+            return keep.tile([P, raw[c0].shape[2] * PACK], BF16, name="grouped%d" % c0, tag=tag, align_bytes=64)
+
+        def quantize(c0, grouped):
+            n = raw[c0].shape[2]
+            c, a = divmod(c0, CHUNK)
+            nc.vector.quantize_mx(out=codes[c][:, a : a + n].bitcast(FP8X4), scales=scales[c][:, a : a + n], in_=grouped[:])
+
+        values = {}
+
+        def layer(c, k, tag=None):
+            acc = psum.tile([P, CHUNK], F32, name="acc%d_%d" % (c, k))
+            cols = slice(k * P, (k + 1) * P)
+            nc.tensor.matmul_mx(
+                out=acc[:],
+                lhsT=w_codes[:, cols].bitcast(FP8X4),
+                lhsT_scale=w_scales[:, cols],
+                rhs=codes[c][:].bitcast(FP8X4),
+                rhs_scale=scales[c][:],
+                start=True,
+                stop=True,
+            )
+            name = "y%d_%d" % (c, k)
+            y = keep.tile([P, CHUNK], F32, name=name, tag=tag or name, align_bytes=64)
+            nc.scalar.activation(out=y[:], in_=acc[:], func=GELU, bias=bias[k][:])
+            values[(c, k)] = y
+
+        def place(c, k):
+            cols = CHUNK // 16
+            nc.vector.tensor_tensor(
+                windows[k][:].indirect(offsets[:, c * cols : (c + 1) * cols]), values[(c, k)][:], gates[c][:], MULT
+            )
+
+        def store(k, c0, c1):
+            nc.sync.dma_start(out[k * P : (k + 1) * P, c0:c1], windows[k][:, c0:c1])
+
+        clear(0)
+        g = new_grouped(0, "g0")
+        interleave(vec, raw[0], g, 0, 256)
+        quantize(0, g)
+        interleave(vec, w_raw, w_grouped, 0, N)
+        nc.vector.quantize_mx(out=w_codes[:].bitcast(FP8X4), scales=w_scales[:], in_=w_grouped[:])
+        g = new_grouped(256, "g256")
+        interleave(vec, raw[256], g, 0, 128)
+        interleave(act, raw[256], g, 128, 256)
+        quantize(256, g)
+        layer(0, 0, "hold2")
+        place(0, 0)
+        clear(1)
+        layer(0, 1)
+
+        def spread(c0, tag):
+            g = new_grouped(c0, tag)
+            for a in range(0, raw[c0].shape[2], 128):
+                interleave(act, raw[c0], g, a, a + 128)
+            quantize(c0, g)
+
+        spread(512, "g512")
+        place(0, 1)
+        layer(1, 0, "hold3")
+        place(1, 0)
+        store(0, 0, 1024)
+        layer(1, 1)
+        place(1, 1)
+        store(1, 0, 1024)
+        spread(1024, "hold2")
+        layer(2, 0)
+        layer(2, 1)
+        place(2, 0)
+        spread(1536, "hold3")
+        spread(1792, "g1792")
+        layer(3, 0)
+        place(3, 0)
+        store(0, 1024, T)
+        place(2, 1)
+        layer(3, 1)
+        place(3, 1)
+        store(1, 1024, T)

@@ -19,6 +19,7 @@ P = 128
 PACK = 4
 CHUNK = 512
 CHUNKS = S // CHUNK
+GROUP = 256
 BLOCKS = N // P
 
 
@@ -27,6 +28,7 @@ def tile_picked_place_lin_gelu_srt_l_kernel(tc, xT, w, b, gate, offs, out):
     with ExitStack() as ctx:
         lists = ctx.enter_context(tc.tile_pool(name="lists", bufs=1))
         keep = ctx.enter_context(tc.tile_pool(name="keep", bufs=1))
+        ring = ctx.enter_context(tc.tile_pool(name="ring", bufs=2))
         psum = ctx.enter_context(tc.psum_pool(name="psum", bufs=1))
 
         offsets = lists.tile([P, S // 16], U16, name="offsets")
@@ -34,10 +36,12 @@ def tile_picked_place_lin_gelu_srt_l_kernel(tc, xT, w, b, gate, offs, out):
         x_hbm = xT.rearrange("(p t) s -> p t s", t=PACK)
         w_hbm = w.rearrange("(p t) m -> p t m", t=PACK)
 
-        pieces = [(0, 256), (256, 256), (512, 512), (1024, 512), (1536, 256), (1792, 256)]
-        raw = {c0: keep.tile([P, PACK, n], F32, name="raw%d" % c0) for c0, n in pieces}
+        loads = [(0, 256), (256, 256), (512, 512), (1024, 512), (1536, 512)]
+        raw = {c0: keep.tile([P, PACK, n], F32, name="raw%d" % c0) for c0, n in loads}
         codes = [keep.tile([P, CHUNK], U32, name="codes%d" % c, align_bytes=64) for c in range(CHUNKS)]
         scales = [keep.tile([P, CHUNK], U8, name="scales%d" % c, align_bytes=64) for c in range(CHUNKS)]
+        values = [[keep.tile([P, CHUNK], F32, name="values%d_%d" % (c, k)) for k in range(BLOCKS)] for c in range(CHUNKS)]
+        sums = [[psum.tile([P, CHUNK], F32, name="sums%d_%d" % (c, k)) for k in range(BLOCKS)] for c in range(CHUNKS)]
         gates = [keep.tile([P, CHUNK], F32, name="gate%d" % c) for c in range(CHUNKS)]
         w_raw = keep.tile([P, PACK, N], F32, name="w_raw")
         w_grouped = keep.tile([P, N * PACK], BF16, name="w_grouped", align_bytes=64)
@@ -59,13 +63,9 @@ def tile_picked_place_lin_gelu_srt_l_kernel(tc, xT, w, b, gate, offs, out):
         load_x(256)
         nc.sync.dma_start(offsets[:], offs)
         load_gate(0)
-        load_x(512)
-        load_gate(1)
-        load_x(1024)
-        load_gate(2)
-        load_x(1536)
-        load_x(1792)
-        load_gate(3)
+        for c in range(1, CHUNKS):
+            load_x(c * CHUNK)
+            load_gate(c)
         for k in range(BLOCKS):
             nc.scalar.dma_start(bias[k][:], b[k * P : (k + 1) * P, :])
 
@@ -76,93 +76,88 @@ def tile_picked_place_lin_gelu_srt_l_kernel(tc, xT, w, b, gate, offs, out):
             for q in range(4):
                 nc.vector.memset(windows[k][:, q * 1024 : (q + 1) * 1024], 0.0)
 
-        def interleave(copy, src, dst, a, e):
-            copy(
-                dst[:, PACK * a : PACK * e].rearrange("p (c i t) -> p c t i", i=4, t=PACK),
-                src[:, :, a:e].rearrange("p t (c i) -> p c t i", i=4),
+        def interleave(src, dst, engines):
+            n = dst.shape[1] // PACK // len(engines)
+            for i, engine in enumerate(engines):
+                source = src[:, :, i * n : (i + 1) * n].rearrange("p t (c i) -> p c t i", i=4)
+                target = dst[:, PACK * i * n : PACK * (i + 1) * n].rearrange("p (c i t) -> p c t i", i=4, t=PACK)
+                if engine == "V":
+                    nc.vector.tensor_copy(out=target, in_=source)
+                else:
+                    nc.scalar.copy(out=target, in_=source)
+
+        grouped = {}
+
+        def spread(g, engines):
+            c0 = g * GROUP
+            start = c0 if c0 in raw else c0 - GROUP
+            grouped[g] = ring.tile([P, GROUP * PACK], BF16, name="grouped", align_bytes=64)
+            interleave(raw[start][:, :, c0 - start : c0 - start + GROUP], grouped[g], engines)
+
+        def quantize(g):
+            c, a = divmod(g * GROUP, CHUNK)
+            nc.vector.quantize_mx(
+                out=codes[c][:, a : a + GROUP].bitcast(FP8X4), scales=scales[c][:, a : a + GROUP], in_=grouped[g][:]
             )
 
-        def vec(dst, src):
-            nc.vector.tensor_copy(out=dst, in_=src)
-
-        def act(dst, src):
-            nc.scalar.copy(out=dst, in_=src)
-
-        def new_grouped(c0, tag):
-            return keep.tile([P, raw[c0].shape[2] * PACK], BF16, name="grouped%d" % c0, tag=tag, align_bytes=64)
-
-        def quantize(c0, grouped):
-            n = raw[c0].shape[2]
-            c, a = divmod(c0, CHUNK)
-            nc.vector.quantize_mx(out=codes[c][:, a : a + n].bitcast(FP8X4), scales=scales[c][:, a : a + n], in_=grouped[:])
-
-        values = {}
-
-        def layer(c, k, tag=None):
-            acc = psum.tile([P, CHUNK], F32, name="acc%d_%d" % (c, k))
-            cols = slice(k * P, (k + 1) * P)
+        def layer(c, k, a=0, n=CHUNK):
+            mine = slice(k * P, (k + 1) * P)
+            cols = slice(a, a + n)
             nc.tensor.matmul_mx(
-                out=acc[:],
-                lhsT=w_codes[:, cols].bitcast(FP8X4),
-                lhsT_scale=w_scales[:, cols],
-                rhs=codes[c][:].bitcast(FP8X4),
-                rhs_scale=scales[c][:],
+                out=sums[c][k][:, cols],
+                lhsT=w_codes[:, mine].bitcast(FP8X4),
+                lhsT_scale=w_scales[:, mine],
+                rhs=codes[c][:, cols].bitcast(FP8X4),
+                rhs_scale=scales[c][:, cols],
                 start=True,
                 stop=True,
             )
-            name = "y%d_%d" % (c, k)
-            y = keep.tile([P, CHUNK], F32, name=name, tag=tag or name, align_bytes=64)
-            nc.scalar.activation(out=y[:], in_=acc[:], func=GELU, bias=bias[k][:])
-            values[(c, k)] = y
+            nc.scalar.activation(out=values[c][k][:, cols], in_=sums[c][k][:, cols], func=GELU, bias=bias[k][:])
 
         def place(c, k):
-            cols = CHUNK // 16
+            n = CHUNK // 16
             nc.vector.tensor_tensor(
-                windows[k][:].indirect(offsets[:, c * cols : (c + 1) * cols]), values[(c, k)][:], gates[c][:], MULT
+                windows[k][:].indirect(offsets[:, c * n : (c + 1) * n]), values[c][k][:], gates[c][:], MULT
             )
 
         def store(k, c0, c1):
             nc.sync.dma_start(out[k * P : (k + 1) * P, c0:c1], windows[k][:, c0:c1])
 
         clear(0)
-        g = new_grouped(0, "g0")
-        interleave(vec, raw[0], g, 0, 256)
-        quantize(0, g)
-        interleave(vec, w_raw, w_grouped, 0, N)
+        spread(0, "SV")
+        interleave(w_raw, w_grouped, "SS")
+        quantize(0)
+        spread(1, "SS")
         nc.vector.quantize_mx(out=w_codes[:].bitcast(FP8X4), scales=w_scales[:], in_=w_grouped[:])
-        g = new_grouped(256, "g256")
-        interleave(vec, raw[256], g, 0, 128)
-        interleave(act, raw[256], g, 128, 256)
-        quantize(256, g)
-        layer(0, 0, "hold2")
-        place(0, 0)
+        quantize(1)
         clear(1)
-        layer(0, 1)
-
-        def spread(c0, tag):
-            g = new_grouped(c0, tag)
-            for a in range(0, raw[c0].shape[2], 128):
-                interleave(act, raw[c0], g, a, a + 128)
-            quantize(c0, g)
-
-        spread(512, "g512")
-        place(0, 1)
-        layer(1, 0, "hold3")
+        for k in range(BLOCKS):
+            for a in (0, GROUP):
+                layer(0, k, a, GROUP)
+        spread(2, "VS")
+        spread(3, "SS")
+        quantize(2)
+        quantize(3)
+        place(0, 0)
+        layer(1, 0)
         place(1, 0)
         store(0, 0, 1024)
+        place(0, 1)
         layer(1, 1)
         place(1, 1)
         store(1, 0, 1024)
-        spread(1024, "hold2")
+        spread(4, "S")
+        spread(5, "S")
+        quantize(4)
+        quantize(5)
         layer(2, 0)
         layer(2, 1)
-        place(2, 0)
-        spread(1536, "hold3")
-        spread(1792, "g1792")
-        layer(3, 0)
-        place(3, 0)
-        store(0, 1024, T)
-        place(2, 1)
-        layer(3, 1)
-        place(3, 1)
-        store(1, 1024, T)
+        spread(6, "VS")
+        spread(7, "VS")
+        quantize(6)
+        quantize(7)
+        for k in range(BLOCKS):
+            place(2, k)
+            layer(3, k)
+            place(3, k)
+            store(k, 1024, T)

from contextlib import ExitStack

import concourse.mybir as mybir

K, T, S, N = 512, 4096, 2048, 256
FLOPS = 2 * K * S * N
BYTES = 4 * (K * S + K * N + N + S + N * T) + 2 * S

F32 = mybir.dt.float32
BF16 = mybir.dt.bfloat16
U32 = mybir.dt.uint32
U16 = mybir.dt.uint16
U8 = mybir.dt.uint8
FP8X4 = mybir.dt.float8_e4m3fn_x4
GELU = mybir.ActivationFunctionType.Gelu_apprx_tanh
MULT = mybir.AluOpType.mult

P = 128
PACK = 4
CHUNK = 512
CHUNKS = S // CHUNK
GROUP = 256
BLOCKS = N // P


def tile_picked_place_lin_gelu_srt_l_kernel(tc, xT, w, b, gate, offs, out):
    nc = tc.nc
    with ExitStack() as ctx:
        lists = ctx.enter_context(tc.tile_pool(name="lists", bufs=1))
        keep = ctx.enter_context(tc.tile_pool(name="keep", bufs=1))
        ring = ctx.enter_context(tc.tile_pool(name="ring", bufs=2))
        psum = ctx.enter_context(tc.psum_pool(name="psum", bufs=1))

        offsets = lists.tile([P, S // 16], U16, name="offsets")

        x_hbm = xT.rearrange("(p t) s -> p t s", t=PACK)
        w_hbm = w.rearrange("(p t) m -> p t m", t=PACK)

        loads = [(0, 256), (256, 256), (512, 512), (1024, 512), (1536, 512)]
        raw = {c0: keep.tile([P, PACK, n], F32, name="raw%d" % c0) for c0, n in loads}
        codes = [keep.tile([P, CHUNK], U32, name="codes%d" % c, align_bytes=64) for c in range(CHUNKS)]
        scales = [keep.tile([P, CHUNK], U8, name="scales%d" % c, align_bytes=64) for c in range(CHUNKS)]
        values = [[keep.tile([P, CHUNK], F32, name="values%d_%d" % (c, k)) for k in range(BLOCKS)] for c in range(CHUNKS)]
        sums = [[psum.tile([P, CHUNK], F32, name="sums%d_%d" % (c, k)) for k in range(BLOCKS)] for c in range(CHUNKS)]
        gates = [keep.tile([P, CHUNK], F32, name="gate%d" % c) for c in range(CHUNKS)]
        w_raw = keep.tile([P, PACK, N], F32, name="w_raw")
        w_grouped = keep.tile([P, N * PACK], BF16, name="w_grouped", align_bytes=64)
        w_codes = keep.tile([P, N], U32, name="w_codes", align_bytes=64)
        w_scales = keep.tile([P, N], U8, name="w_scales", align_bytes=64)
        bias = [keep.tile([P, 1], F32, name="bias%d" % k) for k in range(BLOCKS)]
        windows = [keep.tile([P, T], F32, name="window%d" % k) for k in range(BLOCKS)]
        small = keep.tile([P, 2], F32, name="small")

        def load_x(c0):
            n = raw[c0].shape[2]
            nc.sync.dma_start(raw[c0][:], x_hbm[:, :, c0 : c0 + n])

        def load_gate(c):
            nc.sync.dma_start(gates[c][:], gate[0:P, c * CHUNK : (c + 1) * CHUNK])

        load_x(0)
        nc.sync.dma_start(w_raw[:], w_hbm)
        load_x(256)
        nc.sync.dma_start(offsets[:], offs)
        load_gate(0)
        for c in range(1, CHUNKS):
            load_x(c * CHUNK)
            load_gate(c)
        for k in range(BLOCKS):
            nc.scalar.dma_start(bias[k][:], b[k * P : (k + 1) * P, :])

        nc.gpsimd.memset(small[:, 0:1], 0.0)
        nc.scalar.activation(out=small[:, 1:2], in_=small[:, 0:1], func=GELU)

        def clear(k):
            for q in range(4):
                nc.vector.memset(windows[k][:, q * 1024 : (q + 1) * 1024], 0.0)

        def interleave(src, dst, engines):
            n = dst.shape[1] // PACK // len(engines)
            for i, engine in enumerate(engines):
                source = src[:, :, i * n : (i + 1) * n].rearrange("p t (c i) -> p c t i", i=4)
                target = dst[:, PACK * i * n : PACK * (i + 1) * n].rearrange("p (c i t) -> p c t i", i=4, t=PACK)
                if engine == "V":
                    nc.vector.tensor_copy(out=target, in_=source)
                else:
                    nc.scalar.copy(out=target, in_=source)

        grouped = {}

        def spread(g, engines):
            c0 = g * GROUP
            start = c0 if c0 in raw else c0 - GROUP
            grouped[g] = ring.tile([P, GROUP * PACK], BF16, name="grouped", align_bytes=64)
            interleave(raw[start][:, :, c0 - start : c0 - start + GROUP], grouped[g], engines)

        def quantize(g):
            c, a = divmod(g * GROUP, CHUNK)
            nc.vector.quantize_mx(
                out=codes[c][:, a : a + GROUP].bitcast(FP8X4), scales=scales[c][:, a : a + GROUP], in_=grouped[g][:]
            )

        def layer(c, k, a=0, n=CHUNK):
            mine = slice(k * P, (k + 1) * P)
            cols = slice(a, a + n)
            nc.tensor.matmul_mx(
                out=sums[c][k][:, cols],
                lhsT=w_codes[:, mine].bitcast(FP8X4),
                lhsT_scale=w_scales[:, mine],
                rhs=codes[c][:, cols].bitcast(FP8X4),
                rhs_scale=scales[c][:, cols],
                start=True,
                stop=True,
            )
            nc.scalar.activation(out=values[c][k][:, cols], in_=sums[c][k][:, cols], func=GELU, bias=bias[k][:])

        def place(c, k):
            n = CHUNK // 16
            nc.vector.tensor_tensor(
                windows[k][:].indirect(offsets[:, c * n : (c + 1) * n]), values[c][k][:], gates[c][:], MULT
            )

        def store(k, c0, c1):
            nc.sync.dma_start(out[k * P : (k + 1) * P, c0:c1], windows[k][:, c0:c1])

        clear(0)
        spread(0, "SV")
        interleave(w_raw, w_grouped, "SS")
        quantize(0)
        spread(1, "SS")
        nc.vector.quantize_mx(out=w_codes[:].bitcast(FP8X4), scales=w_scales[:], in_=w_grouped[:])
        quantize(1)
        clear(1)
        for k in range(BLOCKS):
            for a in (0, GROUP):
                layer(0, k, a, GROUP)
        spread(2, "VS")
        spread(3, "SS")
        quantize(2)
        quantize(3)
        place(0, 0)
        layer(1, 0)
        place(1, 0)
        store(0, 0, 1024)
        place(0, 1)
        layer(1, 1)
        place(1, 1)
        store(1, 0, 1024)
        spread(4, "S")
        spread(5, "S")
        quantize(4)
        quantize(5)
        layer(2, 0)
        layer(2, 1)
        spread(6, "VS")
        spread(7, "VS")
        quantize(6)
        quantize(7)
        for k in range(BLOCKS):
            place(2, k)
            layer(3, k)
            place(3, k)
            store(k, 1024, T)
